import numpy as np
import ml_dtypes


def mxq(x, axis, fmt="e4m3"):
    dtype, down = {"e4m3": (ml_dtypes.float8_e4m3fn, 7), "e5m2": (ml_dtypes.float8_e5m2, 14)}[fmt]
    v = np.moveaxis(np.asarray(x, np.float32).astype(ml_dtypes.bfloat16).astype(np.float64), axis, -1)
    blocks = v.reshape(v.shape[:-1] + (-1, 32))
    amax = np.abs(blocks).max(-1, keepdims=True)
    byte = np.maximum(np.where(amax > 0, np.frexp(amax)[1] - 1 + 127, 0) - down, 1)
    scale = np.exp2(byte - 127.0)
    codes = (blocks / scale).astype(np.float32).astype(dtype).astype(np.float64)
    return np.moveaxis((codes * scale).reshape(v.shape), -1, axis)


WIDE = False


def mx_kscale(k):
    if not WIDE:
        return np.ones(k)
    levels = np.array([10, -10, 5, -5, 0])
    if k % 512:
        return np.exp2(np.random.permutation(np.resize(levels, k // 32))).repeat(32)
    a = np.empty((k // 512, 16))
    for p in range(k // 512):
        a[p, :8] = np.random.permutation(np.resize(levels, 8))
        for g in range(8):
            far = levels[np.abs(levels - a[p, g]) >= 10]
            a[p, g + 8] = far[np.random.randint(len(far))]
    return np.exp2(a.ravel()).repeat(32)


def f64(x):
    return np.asarray(x).astype(np.float64)


def striped(idx):
    return np.tile(idx.reshape(-1, 16).T, (8, 1)).astype(np.uint16)


def unstriped(offs):
    return offs[:16].T.reshape(-1).astype(np.int64)


def relu(v):
    return np.maximum(v, 0.0)


K, T, S, H, N = 512, 2048, 1024, 512, 512


def setup_inputs():
    n = np.random.standard_normal
    s = mx_kscale(K)[:, None]
    u = mx_kscale(H)
    return {
        "xT": (n((K, S)) * s).astype(np.float32),
        "w1": (n((K, H)) / np.sqrt(K) / s * u).astype(np.float32),
        "w2": (n((H, N)) / np.sqrt(H) / u[:, None]).astype(np.float32),
        "gate": np.tile(np.random.uniform(0.2, 1.0, S), (N, 1)).astype(np.float32),
        "offs": striped(np.random.permutation(T)[:S]),
    }


def reference(xT, w1, w2, gate, offs):
    idx = unstriped(offs)
    xq = mxq(f64(xT), 0, "e4m3")
    h = relu(mxq(f64(w1), 0, "e4m3").T @ xq)
    y = mxq(f64(w2), 0, "e4m3").T @ mxq(h, 0, "e4m3")
    out = np.zeros((N, T))
    out[:, idx] = f64(gate) * y
    return out

@@ -1,0 +1,188 @@
+from contextlib import ExitStack
+
+import concourse.mybir as mybir
+
+P = 128
+K, S, H, N, T = 512, 1024, 512, 512, 2048
+PACK = 4
+
+FLOPS = 2 * S * H * (K + N)
+BYTES = 4 * (K * S + K * H + H * N + S + N * T) + 2 * P * (S // 16)
+
+F32 = mybir.dt.float32
+BF16 = mybir.dt.bfloat16
+U32 = mybir.dt.uint32
+U16 = mybir.dt.uint16
+U8 = mybir.dt.uint8
+FP8X4 = mybir.dt.float8_e4m3fn_x4
+RELU = mybir.ActivationFunctionType.Relu
+MULT = mybir.AluOpType.mult
+
+SUB = 128
+CHUNKS = ((0, 256), (256, 256), (512, 512))
+
+
+def tile_picked_place_mlp_relu_sub_l_kernel(tc, xT, w1, w2, gate, offs, out):
+    nc = tc.nc
+    blocks = N // P
+
+    with ExitStack() as ctx:
+        keep = ctx.enter_context(tc.tile_pool(name="keep", bufs=1))
+        psum1 = ctx.enter_context(tc.psum_pool(name="psum1", bufs=4))
+        psum2 = ctx.enter_context(tc.psum_pool(name="psum2", bufs=4))
+
+        offsets = keep.tile([P, S // 16], U16, name="offsets")
+        w1_raw = keep.tile([P, PACK, H], F32, name="w1_raw")
+        x_raw = [keep.tile([P, PACK, n], F32, name=f"x_raw{c}") for c, (s, n) in enumerate(CHUNKS)]
+        w2_raw = [keep.tile([P, PACK, N // 2], F32, name=f"w2_raw{i}") for i in range(2)]
+        gates = [keep.tile([P, n], F32, name=f"gate{c}") for c, (s, n) in enumerate(CHUNKS)]
+
+        w1_bf = keep.tile([P, PACK, P, PACK], BF16, name="w1_bf", align_bytes=64)
+        w1_codes = keep.tile([P, H], U32, name="w1_codes", align_bytes=64)
+        w1_scales = keep.tile([P, H], U8, name="w1_scales", align_bytes=64)
+        w2_bf = keep.tile([P, N, PACK], BF16, name="w2_bf", align_bytes=64)
+        w2_codes = keep.tile([P, N], U32, name="w2_codes", align_bytes=64)
+        w2_scales = keep.tile([P, N], U8, name="w2_scales", align_bytes=64)
+        x_bf = keep.tile([P, S, PACK], BF16, name="x_bf", align_bytes=64)
+        x_codes = keep.tile([P, S], U32, name="x_codes", align_bytes=64)
+        x_scales = keep.tile([P, S], U8, name="x_scales", align_bytes=64)
+        h_bf = keep.tile([P, S, PACK], BF16, name="h_bf", align_bytes=64)
+        h_codes = keep.tile([P, S], U32, name="h_codes", align_bytes=64)
+        h_scales = keep.tile([P, S], U8, name="h_scales", align_bytes=64)
+        y = [keep.tile([P, S], F32, name=f"y{b}") for b in range(blocks)]
+        window = [keep.tile([P, T], F32, name=f"window{b}") for b in range(blocks)]
+        warm = keep.tile([P, 2], F32, name="warm")
+
+        def load_x(c):
+            s, n = CHUNKS[c]
+            nc.sync.dma_start(x_raw[c][:], xT[:, s : s + n].rearrange("(p j) w -> p j w", j=PACK))
+
+        def load_gate(c):
+            s, n = CHUNKS[c]
+            nc.sync.dma_start(gates[c][:], gate[0:P, s : s + n])
+
+        def load_w2(i):
+            nc.sync.dma_start(w2_raw[i][:], w2[:, i * N // 2 : (i + 1) * N // 2].rearrange("(p j) w -> p j w", j=PACK))
+
+        nc.sync.dma_start(w1_raw[:], w1.rearrange("(p j) w -> p j w", j=PACK))
+        load_x(0)
+        load_w2(0)
+        nc.sync.dma_start(offsets[:], offs)
+        load_gate(0)
+        load_w2(1)
+        load_x(1)
+        load_gate(1)
+        load_x(2)
+        load_gate(2)
+
+        nc.gpsimd.memset(warm[:], 0.0)
+        nc.scalar.activation(warm[:, 1:2], warm[:, 0:1], RELU)
+        for b in range(blocks):
+            nc.vector.memset(window[b][:], 0.0)
+
+        def quantise(codes, scales, grouped, s, n):
+            nc.vector.quantize_mx(
+                out=codes[:, s : s + n].bitcast(FP8X4),
+                scales=scales[:, s : s + n],
+                in_=grouped[:, s : s + n, :].rearrange("p w j -> p (w j)"),
+            )
+
+        def interleave(copy, grouped, raw, s, r, n):
+            copy(
+                grouped[:, s : s + n, :].rearrange("p (c i) j -> p c j i", i=4),
+                raw[:, :, r : r + n].rearrange("p j (c i) -> p c j i", i=4),
+            )
+
+        w1_view = w1_raw[:].rearrange("p j (m t) -> p m t j", t=PACK)
+        w1_flat = w1_bf[:].rearrange("p t m j -> p (t m) j")
+        nc.vector.tensor_copy(w1_bf[:, 0:2].rearrange("p t m j -> p m t j"), w1_view[:, :, 0:2, :])
+        nc.scalar.copy(w1_bf[:, 3], w1_view[:, :, 3, :])
+        nc.vector.tensor_copy(w1_bf[:, 2], w1_view[:, :, 2, :])
+        quantise(w1_codes, w1_scales, w1_flat, 0, 2 * P)
+        quantise(w1_codes, w1_scales, w1_flat, 2 * P, 2 * P)
+
+        def hidden(s):
+            acc = psum1.tile([P, PACK, SUB], F32, name="hidden_acc")
+            for t in range(PACK):
+                nc.tensor.matmul_mx(
+                    out=acc[:, t, :],
+                    lhsT=w1_codes[:, t * P : (t + 1) * P].bitcast(FP8X4),
+                    lhsT_scale=w1_scales[:, t * P : (t + 1) * P],
+                    rhs=x_codes[:, s : s + SUB].bitcast(FP8X4),
+                    rhs_scale=x_scales[:, s : s + SUB],
+                    start=True,
+                    stop=True,
+                )
+            return acc
+
+        def relu(acc, s):
+            nc.scalar.activation(h_bf[:, s : s + SUB, :], acc[:].rearrange("p t w -> p w t"), RELU)
+
+        def product(b, c):
+            s, n = CHUNKS[c]
+            acc = psum2.tile([P, 512], F32, name="out_acc")
+            nc.tensor.matmul_mx(
+                out=acc[:, 0:n],
+                lhsT=w2_codes[:, b * P : (b + 1) * P].bitcast(FP8X4),
+                lhsT_scale=w2_scales[:, b * P : (b + 1) * P],
+                rhs=h_codes[:, s : s + n].bitcast(FP8X4),
+                rhs_scale=h_scales[:, s : s + n],
+                start=True,
+                stop=True,
+            )
+            nc.scalar.copy(y[b][:, s : s + n], acc[:, 0:n])
+
+        def scatter(b, c):
+            s, n = CHUNKS[c]
+            nc.vector.tensor_tensor(
+                window[b][:].indirect(offsets[:, s // 16 : (s + n) // 16]), y[b][:, s : s + n], gates[c][:], MULT
+            )
+
+        interleave(nc.vector.tensor_copy, x_bf, x_raw[0], 0, 0, SUB)
+        interleave(nc.scalar.copy, x_bf, x_raw[0], SUB, SUB, SUB)
+        quantise(x_codes, x_scales, x_bf, 0, SUB)
+        quantise(x_codes, x_scales, x_bf, SUB, SUB)
+        acc_a = hidden(0)
+        acc_b = hidden(SUB)
+        relu(acc_a, 0)
+        relu(acc_b, SUB)
+        for i in range(2):
+            interleave(nc.vector.tensor_copy, w2_bf, w2_raw[0], i * P, i * P, P)
+            quantise(w2_codes, w2_scales, w2_bf, i * P, P)
+        quantise(h_codes, h_scales, h_bf, 0, SUB)
+        quantise(h_codes, h_scales, h_bf, SUB, SUB)
+        product(0, 0)
+        product(1, 0)
+        scatter(0, 0)
+
+        for i in range(2):
+            interleave(nc.scalar.copy, w2_bf, w2_raw[1], N // 2 + i * P, i * P, P)
+        quantise(w2_codes, w2_scales, w2_bf, N // 2, N // 2)
+        for i in range(2):
+            interleave(nc.scalar.copy, x_bf, x_raw[1], 256 + i * SUB, i * SUB, SUB)
+        product(2, 0)
+        product(3, 0)
+        scatter(1, 0)
+        quantise(x_codes, x_scales, x_bf, 256, 256)
+        for i in range(2):
+            relu(hidden(256 + i * SUB), 256 + i * SUB)
+        scatter(2, 0)
+        quantise(h_codes, h_scales, h_bf, 256, 256)
+        for b in range(blocks):
+            product(b, 1)
+        for i in range(4):
+            interleave(nc.scalar.copy, x_bf, x_raw[2], 512 + i * SUB, i * SUB, SUB)
+        scatter(3, 0)
+        quantise(x_codes, x_scales, x_bf, 512, 512)
+        for i in range(4):
+            relu(hidden(512 + i * SUB), 512 + i * SUB)
+        scatter(0, 1)
+        scatter(1, 1)
+        quantise(h_codes, h_scales, h_bf, 512, 512)
+        for b in range(blocks):
+            product(b, 2)
+        scatter(2, 1)
+        scatter(3, 1)
+        for b in range(blocks):
+            scatter(b, 2)
+            nc.sync.dma_start(out[b * P : (b + 1) * P, :], window[b][:])

@@ -3,8 +3,12 @@ from contextlib import ExitStack
 import concourse.mybir as mybir
 
 P = 128
-K, S, H, N, T = 512, 1024, 512, 512, 2048
 PACK = 4
+K, S, H, N, T = 512, 1024, 512, 512, 2048
+BLOCKS = N // P
+CHUNK = 256
+HALF = CHUNK // 2
+BANK = 512
 
 FLOPS = 2 * S * H * (K + N)
 BYTES = 4 * (K * S + K * H + H * N + S + N * T) + 2 * P * (S // 16)
@@ -18,109 +22,118 @@ FP8X4 = mybir.dt.float8_e4m3fn_x4
 RELU = mybir.ActivationFunctionType.Relu
 MULT = mybir.AluOpType.mult
 
-SUB = 128
-CHUNKS = ((0, 256), (256, 256), (512, 512))
+
+def rows_by_four(dram):
+    return dram.rearrange("(p t) w -> p t w", t=PACK)
 
 
 def tile_picked_place_mlp_relu_sub_l_kernel(tc, xT, w1, w2, gate, offs, out):
     nc = tc.nc
-    blocks = N // P
 
     with ExitStack() as ctx:
-        keep = ctx.enter_context(tc.tile_pool(name="keep", bufs=1))
-        psum1 = ctx.enter_context(tc.psum_pool(name="psum1", bufs=4))
-        psum2 = ctx.enter_context(tc.psum_pool(name="psum2", bufs=4))
+        held = ctx.enter_context(tc.tile_pool(name="held", bufs=1))
+        hidden_psum = ctx.enter_context(tc.psum_pool(name="hidden_psum", bufs=4))
+        out_psum = ctx.enter_context(tc.psum_pool(name="out_psum", bufs=4))
 
-        offsets = keep.tile([P, S // 16], U16, name="offsets")
-        w1_raw = keep.tile([P, PACK, H], F32, name="w1_raw")
-        x_raw = [keep.tile([P, PACK, n], F32, name=f"x_raw{c}") for c, (s, n) in enumerate(CHUNKS)]
-        w2_raw = [keep.tile([P, PACK, N // 2], F32, name=f"w2_raw{i}") for i in range(2)]
-        gates = [keep.tile([P, n], F32, name=f"gate{c}") for c, (s, n) in enumerate(CHUNKS)]
+        offsets = held.tile([P, S // 16], U16, name="offsets")
+        x_raw = [held.tile([P, PACK, CHUNK], F32, name=f"x_raw{c}", tag=f"x_bytes{c}") for c in range(S // CHUNK)]
+        w1_raw = held.tile([P, PACK, H], F32, name="w1_raw")
+        w2_raw = [held.tile([P, PACK, N // 2], F32, name=f"w2_raw{i}") for i in range(2)]
+        gates = held.tile([P, S], F32, name="gates")
 
-        w1_bf = keep.tile([P, PACK, P, PACK], BF16, name="w1_bf", align_bytes=64)
-        w1_codes = keep.tile([P, H], U32, name="w1_codes", align_bytes=64)
-        w1_scales = keep.tile([P, H], U8, name="w1_scales", align_bytes=64)
-        w2_bf = keep.tile([P, N, PACK], BF16, name="w2_bf", align_bytes=64)
-        w2_codes = keep.tile([P, N], U32, name="w2_codes", align_bytes=64)
-        w2_scales = keep.tile([P, N], U8, name="w2_scales", align_bytes=64)
-        x_bf = keep.tile([P, S, PACK], BF16, name="x_bf", align_bytes=64)
-        x_codes = keep.tile([P, S], U32, name="x_codes", align_bytes=64)
-        x_scales = keep.tile([P, S], U8, name="x_scales", align_bytes=64)
-        h_bf = keep.tile([P, S, PACK], BF16, name="h_bf", align_bytes=64)
-        h_codes = keep.tile([P, S], U32, name="h_codes", align_bytes=64)
-        h_scales = keep.tile([P, S], U8, name="h_scales", align_bytes=64)
-        y = [keep.tile([P, S], F32, name=f"y{b}") for b in range(blocks)]
-        window = [keep.tile([P, T], F32, name=f"window{b}") for b in range(blocks)]
-        warm = keep.tile([P, 2], F32, name="warm")
+        w1_bf = held.tile([P, PACK, P, PACK], BF16, name="w1_bf", align_bytes=64)
+        w1_codes = held.tile([P, H], U32, name="w1_codes", align_bytes=64)
+        w1_scales = held.tile([P, H], U8, name="w1_scales", align_bytes=64)
+        w2_bf = held.tile([P, N, PACK], BF16, name="w2_bf", align_bytes=64)
+        w2_codes = held.tile([P, N], U32, name="w2_codes", align_bytes=64)
+        w2_scales = held.tile([P, N], U8, name="w2_scales", align_bytes=64)
+        x_bf = held.tile([P, S, PACK], BF16, name="x_bf", align_bytes=64)
+        x_codes = held.tile([P, S], U32, name="x_codes", align_bytes=64)
+        x_scales = held.tile([P, S], U8, name="x_scales", align_bytes=64)
+        h_bf = held.tile([P, S, PACK], BF16, name="h_bf", align_bytes=64)
+        h_codes = held.tile([P, S], U32, name="h_codes", align_bytes=64)
+        h_scales = held.tile([P, S], U8, name="h_scales", align_bytes=64)
+        window = [held.tile([P, T], F32, name=f"window{b}") for b in range(BLOCKS)]
+        zero = held.tile([P, 2], F32, name="zero")
 
         def load_x(c):
-            s, n = CHUNKS[c]
-            nc.sync.dma_start(x_raw[c][:], xT[:, s : s + n].rearrange("(p j) w -> p j w", j=PACK))
-
-        def load_gate(c):
-            s, n = CHUNKS[c]
-            nc.sync.dma_start(gates[c][:], gate[0:P, s : s + n])
+            nc.sync.dma_start(x_raw[c][:], rows_by_four(xT[:, c * CHUNK : (c + 1) * CHUNK]))
 
         def load_w2(i):
-            nc.sync.dma_start(w2_raw[i][:], w2[:, i * N // 2 : (i + 1) * N // 2].rearrange("(p j) w -> p j w", j=PACK))
+            nc.sync.dma_start(w2_raw[i][:], rows_by_four(w2[:, i * N // 2 : (i + 1) * N // 2]))
 
-        nc.sync.dma_start(w1_raw[:], w1.rearrange("(p j) w -> p j w", j=PACK))
+        nc.sync.dma_start(w1_raw[:], rows_by_four(w1))
         load_x(0)
         load_w2(0)
         nc.sync.dma_start(offsets[:], offs)
-        load_gate(0)
+        nc.sync.dma_start(gates[:, 0:CHUNK], gate[0:P, 0:CHUNK])
         load_w2(1)
         load_x(1)
-        load_gate(1)
         load_x(2)
-        load_gate(2)
+        load_x(3)
+        nc.sync.dma_start(gates[:, CHUNK:S], gate[0:P, CHUNK:S])
 
-        nc.gpsimd.memset(warm[:], 0.0)
-        nc.scalar.activation(warm[:, 1:2], warm[:, 0:1], RELU)
-        for b in range(blocks):
-            nc.vector.memset(window[b][:], 0.0)
+        nc.gpsimd.memset(zero[:], 0.0)
+        nc.scalar.activation(zero[:, 1:2], zero[:, 0:1], RELU)
+        nc.gpsimd.memset(window[3][:], 0.0)
+        nc.vector.memset(window[0][:], 0.0)
+        nc.vector.memset(window[1][:], 0.0)
+        nc.scalar.copy(window[2][:, T // 2 :], zero[:, 0:1].to_broadcast([P, T // 2]))
+
+        def interleave(copy, grouped, raw, s, r, n):
+            copy(
+                grouped[:, s : s + n, :].rearrange("p (c i) t -> p c t i", i=4),
+                raw[:, :, r : r + n].rearrange("p t (c i) -> p c t i", i=4),
+            )
 
         def quantise(codes, scales, grouped, s, n):
             nc.vector.quantize_mx(
                 out=codes[:, s : s + n].bitcast(FP8X4),
                 scales=scales[:, s : s + n],
-                in_=grouped[:, s : s + n, :].rearrange("p w j -> p (w j)"),
+                in_=grouped[:, s : s + n, :].rearrange("p w t -> p (w t)"),
             )
 
-        def interleave(copy, grouped, raw, s, r, n):
-            copy(
-                grouped[:, s : s + n, :].rearrange("p (c i) j -> p c j i", i=4),
-                raw[:, :, r : r + n].rearrange("p j (c i) -> p c j i", i=4),
-            )
+        def prepare_x(c):
+            s = c * CHUNK
+            for i in range(2):
+                interleave(nc.scalar.copy, x_bf, x_raw[c], s + i * HALF, i * HALF, HALF)
+            quantise(x_codes, x_scales, x_bf, s, CHUNK)
 
-        w1_view = w1_raw[:].rearrange("p j (m t) -> p m t j", t=PACK)
-        w1_flat = w1_bf[:].rearrange("p t m j -> p (t m) j")
-        nc.vector.tensor_copy(w1_bf[:, 0:2].rearrange("p t m j -> p m t j"), w1_view[:, :, 0:2, :])
-        nc.scalar.copy(w1_bf[:, 3], w1_view[:, :, 3, :])
-        nc.vector.tensor_copy(w1_bf[:, 2], w1_view[:, :, 2, :])
-        quantise(w1_codes, w1_scales, w1_flat, 0, 2 * P)
-        quantise(w1_codes, w1_scales, w1_flat, 2 * P, 2 * P)
+        def prepare_w2(copy, b):
+            interleave(copy, w2_bf, w2_raw[b // 2], b * P, b % 2 * P, P)
+            quantise(w2_codes, w2_scales, w2_bf, b * P, P)
 
         def hidden(s):
-            acc = psum1.tile([P, PACK, SUB], F32, name="hidden_acc")
+            acc = hidden_psum.tile([P, PACK, HALF], F32, name="hidden_acc")
             for t in range(PACK):
                 nc.tensor.matmul_mx(
                     out=acc[:, t, :],
                     lhsT=w1_codes[:, t * P : (t + 1) * P].bitcast(FP8X4),
                     lhsT_scale=w1_scales[:, t * P : (t + 1) * P],
-                    rhs=x_codes[:, s : s + SUB].bitcast(FP8X4),
-                    rhs_scale=x_scales[:, s : s + SUB],
+                    rhs=x_codes[:, s : s + HALF].bitcast(FP8X4),
+                    rhs_scale=x_scales[:, s : s + HALF],
                     start=True,
                     stop=True,
                 )
             return acc
 
-        def relu(acc, s):
-            nc.scalar.activation(h_bf[:, s : s + SUB, :], acc[:].rearrange("p t w -> p w t"), RELU)
+        def relu_on_scalar(acc, s):
+            nc.scalar.activation(h_bf[:, s : s + HALF, :], acc[:].rearrange("p t w -> p w t"), RELU)
 
-        def product(b, c):
-            s, n = CHUNKS[c]
-            acc = psum2.tile([P, 512], F32, name="out_acc")
+        def relu_on_vector(acc, s):
+            nc.vector.tensor_scalar_max(h_bf[:, s : s + HALF, :], acc[:].rearrange("p t w -> p w t"), 0.0)
+
+        def first_layer(c):
+            s = c * CHUNK
+            relu_on_scalar(hidden(s), s)
+            bank = hidden(s + HALF)
+            relu_on_scalar(bank, s + HALF)
+            quantise(h_codes, h_scales, h_bf, s, CHUNK)
+            return bank[:].rearrange("p t w -> p (t w)")
+
+        def second_layer(b, s, n, y, copy=nc.scalar.copy, acc=None):
+            if acc is None:
+                acc = out_psum.tile([P, BANK], F32, name="out_acc")
             nc.tensor.matmul_mx(
                 out=acc[:, 0:n],
                 lhsT=w2_codes[:, b * P : (b + 1) * P].bitcast(FP8X4),
@@ -130,59 +143,73 @@ def tile_picked_place_mlp_relu_sub_l_kernel(tc, xT, w1, w2, gate, offs, out):
                 start=True,
                 stop=True,
             )
-            nc.scalar.copy(y[b][:, s : s + n], acc[:, 0:n])
+            copy(y, acc[:, 0:n])
 
-        def scatter(b, c):
-            s, n = CHUNKS[c]
+        def scatter(b, s, n, y):
             nc.vector.tensor_tensor(
-                window[b][:].indirect(offsets[:, s // 16 : (s + n) // 16]), y[b][:, s : s + n], gates[c][:], MULT
+                window[b][:].indirect(offsets[:, s // 16 : (s + n) // 16]), y, gates[:, s : s + n], MULT
             )
 
-        interleave(nc.vector.tensor_copy, x_bf, x_raw[0], 0, 0, SUB)
-        interleave(nc.scalar.copy, x_bf, x_raw[0], SUB, SUB, SUB)
-        quantise(x_codes, x_scales, x_bf, 0, SUB)
-        quantise(x_codes, x_scales, x_bf, SUB, SUB)
-        acc_a = hidden(0)
-        acc_b = hidden(SUB)
-        relu(acc_a, 0)
-        relu(acc_b, SUB)
-        for i in range(2):
-            interleave(nc.vector.tensor_copy, w2_bf, w2_raw[0], i * P, i * P, P)
-            quantise(w2_codes, w2_scales, w2_bf, i * P, P)
-        quantise(h_codes, h_scales, h_bf, 0, SUB)
-        quantise(h_codes, h_scales, h_bf, SUB, SUB)
-        product(0, 0)
-        product(1, 0)
-        scatter(0, 0)
+        y0 = held.tile([P, S], F32, name="y0")
+        y1_first = held.tile([P, CHUNK], F32, name="y1_first")
+        y2 = held.tile([P, S], F32, name="y2")
 
+        interleave(nc.vector.tensor_copy, x_bf, x_raw[0], 0, 0, HALF)
+        interleave(nc.scalar.copy, x_bf, x_raw[0], HALF, HALF, HALF)
+        quantise(x_codes, x_scales, x_bf, 0, CHUNK)
+        w1_by_slot = w1_raw[:].rearrange("p j (m t) -> p m t j", t=PACK)
+        w1_columns = w1_bf[:].rearrange("p t m j -> p (t m) j")
+        nc.vector.tensor_copy(w1_bf[:, 0:2].rearrange("p t m j -> p m t j"), w1_by_slot[:, :, 0:2, :])
+        nc.scalar.copy(w1_bf[:, 3], w1_by_slot[:, :, 3, :])
+        nc.vector.tensor_copy(w1_bf[:, 2], w1_by_slot[:, :, 2, :])
+        quantise(w1_codes, w1_scales, w1_columns, 0, H // 2)
+        quantise(w1_codes, w1_scales, w1_columns, H // 2, H // 2)
+        halves = [hidden(i * HALF) for i in range(2)]
         for i in range(2):
-            interleave(nc.scalar.copy, w2_bf, w2_raw[1], N // 2 + i * P, i * P, P)
-        quantise(w2_codes, w2_scales, w2_bf, N // 2, N // 2)
+            relu_on_vector(halves[i], i * HALF)
+        prepare_w2(nc.vector.tensor_copy, 0)
         for i in range(2):
-            interleave(nc.scalar.copy, x_bf, x_raw[1], 256 + i * SUB, i * SUB, SUB)
-        product(2, 0)
-        product(3, 0)
-        scatter(1, 0)
-        quantise(x_codes, x_scales, x_bf, 256, 256)
+            quantise(h_codes, h_scales, h_bf, i * HALF, HALF)
         for i in range(2):
-            relu(hidden(256 + i * SUB), 256 + i * SUB)
-        scatter(2, 0)
-        quantise(h_codes, h_scales, h_bf, 256, 256)
-        for b in range(blocks):
-            product(b, 1)
-        for i in range(4):
-            interleave(nc.scalar.copy, x_bf, x_raw[2], 512 + i * SUB, i * SUB, SUB)
-        scatter(3, 0)
-        quantise(x_codes, x_scales, x_bf, 512, 512)
-        for i in range(4):
-            relu(hidden(512 + i * SUB), 512 + i * SUB)
-        scatter(0, 1)
-        scatter(1, 1)
-        quantise(h_codes, h_scales, h_bf, 512, 512)
-        for b in range(blocks):
-            product(b, 2)
-        scatter(2, 1)
-        scatter(3, 1)
-        for b in range(blocks):
-            scatter(b, 2)
+            second_layer(0, i * HALF, HALF, y0[:, i * HALF : (i + 1) * HALF], nc.vector.tensor_copy)
+        nc.vector.memset(window[2][:, : T // 2], 0.0)
+        scatter(0, 0, CHUNK, y0[:, 0:CHUNK])
+
+        prepare_w2(nc.scalar.copy, 1)
+        prepare_x(1)
+        second_layer(1, 0, CHUNK, y1_first[:])
+        scatter(1, 0, CHUNK, y1_first[:])
+        first_layer(1)
+        prepare_w2(nc.scalar.copy, 2)
+        second_layer(2, 0, CHUNK, y2[:, 0:CHUNK])
+        scatter(2, 0, CHUNK, y2[:, 0:CHUNK])
+        prepare_x(2)
+        prepare_w2(nc.scalar.copy, 3)
+        y3 = held.tile([P, S], F32, name="y3", tag="x_bytes2")
+        second_layer(3, 0, CHUNK, y3[:, 0:CHUNK])
+        scatter(3, 0, CHUNK, y3[:, 0:CHUNK])
+
+        second_layer(0, CHUNK, CHUNK, y0[:, CHUNK : 2 * CHUNK])
+        scatter(0, CHUNK, CHUNK, y0[:, CHUNK : 2 * CHUNK])
+        first_layer(2)
+        prepare_x(3)
+        y1 = held.tile([P, S - CHUNK], F32, name="y1", tag="x_bytes3")
+        second_layer(1, CHUNK, CHUNK, y1[:, 0:CHUNK])
+        scatter(1, CHUNK, CHUNK, y1[:, 0:CHUNK])
+        second_layer(2, CHUNK, 2 * CHUNK, y2[:, CHUNK : 3 * CHUNK])
+        scatter(2, CHUNK, 2 * CHUNK, y2[:, CHUNK : 3 * CHUNK])
+        bank = first_layer(3)
+        second_layer(3, CHUNK, 2 * CHUNK, y3[:, CHUNK : 3 * CHUNK], acc=bank)
+        scatter(3, CHUNK, 2 * CHUNK, y3[:, CHUNK : 3 * CHUNK])
+
+        rest = (
+            (2, 3 * CHUNK, CHUNK, y2[:, 3 * CHUNK :]),
+            (3, 3 * CHUNK, CHUNK, y3[:, 3 * CHUNK :]),
+            (0, 2 * CHUNK, 2 * CHUNK, y0[:, 2 * CHUNK :]),
+            (1, 2 * CHUNK, 2 * CHUNK, y1[:, CHUNK:]),
+        )
+        for b, s, n, y in rest:
+            second_layer(b, s, n, y)
+        for b, s, n, y in rest:
+            scatter(b, s, n, y)
             nc.sync.dma_start(out[b * P : (b + 1) * P, :], window[b][:])

from contextlib import ExitStack

import concourse.mybir as mybir

P = 128
PACK = 4
K, S, H, N, T = 512, 1024, 512, 512, 2048
BLOCKS = N // P
CHUNK = 256
HALF = CHUNK // 2
BANK = 512

FLOPS = 2 * S * H * (K + N)
BYTES = 4 * (K * S + K * H + H * N + S + N * T) + 2 * P * (S // 16)

F32 = mybir.dt.float32
BF16 = mybir.dt.bfloat16
U32 = mybir.dt.uint32
U16 = mybir.dt.uint16
U8 = mybir.dt.uint8
FP8X4 = mybir.dt.float8_e4m3fn_x4
RELU = mybir.ActivationFunctionType.Relu
MULT = mybir.AluOpType.mult


def rows_by_four(dram):
    return dram.rearrange("(p t) w -> p t w", t=PACK)


def tile_picked_place_mlp_relu_sub_l_kernel(tc, xT, w1, w2, gate, offs, out):
    nc = tc.nc

    with ExitStack() as ctx:
        held = ctx.enter_context(tc.tile_pool(name="held", bufs=1))
        hidden_psum = ctx.enter_context(tc.psum_pool(name="hidden_psum", bufs=4))
        out_psum = ctx.enter_context(tc.psum_pool(name="out_psum", bufs=4))

        offsets = held.tile([P, S // 16], U16, name="offsets")
        x_raw = [held.tile([P, PACK, CHUNK], F32, name=f"x_raw{c}", tag=f"x_bytes{c}") for c in range(S // CHUNK)]
        w1_raw = held.tile([P, PACK, H], F32, name="w1_raw")
        w2_raw = [held.tile([P, PACK, N // 2], F32, name=f"w2_raw{i}") for i in range(2)]
        gates = held.tile([P, S], F32, name="gates")

        w1_bf = held.tile([P, PACK, P, PACK], BF16, name="w1_bf", align_bytes=64)
        w1_codes = held.tile([P, H], U32, name="w1_codes", align_bytes=64)
        w1_scales = held.tile([P, H], U8, name="w1_scales", align_bytes=64)
        w2_bf = held.tile([P, N, PACK], BF16, name="w2_bf", align_bytes=64)
        w2_codes = held.tile([P, N], U32, name="w2_codes", align_bytes=64)
        w2_scales = held.tile([P, N], U8, name="w2_scales", align_bytes=64)
        x_bf = held.tile([P, S, PACK], BF16, name="x_bf", align_bytes=64)
        x_codes = held.tile([P, S], U32, name="x_codes", align_bytes=64)
        x_scales = held.tile([P, S], U8, name="x_scales", align_bytes=64)
        h_bf = held.tile([P, S, PACK], BF16, name="h_bf", align_bytes=64)
        h_codes = held.tile([P, S], U32, name="h_codes", align_bytes=64)
        h_scales = held.tile([P, S], U8, name="h_scales", align_bytes=64)
        window = [held.tile([P, T], F32, name=f"window{b}") for b in range(BLOCKS)]
        zero = held.tile([P, 2], F32, name="zero")

        def load_x(c):
            nc.sync.dma_start(x_raw[c][:], rows_by_four(xT[:, c * CHUNK : (c + 1) * CHUNK]))

        def load_w2(i):
            nc.sync.dma_start(w2_raw[i][:], rows_by_four(w2[:, i * N // 2 : (i + 1) * N // 2]))

        nc.sync.dma_start(w1_raw[:], rows_by_four(w1))
        load_x(0)
        load_w2(0)
        nc.sync.dma_start(offsets[:], offs)
        nc.sync.dma_start(gates[:, 0:CHUNK], gate[0:P, 0:CHUNK])
        load_w2(1)
        load_x(1)
        load_x(2)
        load_x(3)
        nc.sync.dma_start(gates[:, CHUNK:S], gate[0:P, CHUNK:S])

        nc.gpsimd.memset(zero[:], 0.0)
        nc.scalar.activation(zero[:, 1:2], zero[:, 0:1], RELU)
        nc.gpsimd.memset(window[3][:], 0.0)
        nc.vector.memset(window[0][:], 0.0)
        nc.vector.memset(window[1][:], 0.0)
        nc.scalar.copy(window[2][:, T // 2 :], zero[:, 0:1].to_broadcast([P, T // 2]))

        def interleave(copy, grouped, raw, s, r, n):
            copy(
                grouped[:, s : s + n, :].rearrange("p (c i) t -> p c t i", i=4),
                raw[:, :, r : r + n].rearrange("p t (c i) -> p c t i", i=4),
            )

        def quantise(codes, scales, grouped, s, n):
            nc.vector.quantize_mx(
                out=codes[:, s : s + n].bitcast(FP8X4),
                scales=scales[:, s : s + n],
                in_=grouped[:, s : s + n, :].rearrange("p w t -> p (w t)"),
            )

        def prepare_x(c):
            s = c * CHUNK
            for i in range(2):
                interleave(nc.scalar.copy, x_bf, x_raw[c], s + i * HALF, i * HALF, HALF)
            quantise(x_codes, x_scales, x_bf, s, CHUNK)

        def prepare_w2(copy, b):
            interleave(copy, w2_bf, w2_raw[b // 2], b * P, b % 2 * P, P)
            quantise(w2_codes, w2_scales, w2_bf, b * P, P)

        def hidden(s):
            acc = hidden_psum.tile([P, PACK, HALF], F32, name="hidden_acc")
            for t in range(PACK):
                nc.tensor.matmul_mx(
                    out=acc[:, t, :],
                    lhsT=w1_codes[:, t * P : (t + 1) * P].bitcast(FP8X4),
                    lhsT_scale=w1_scales[:, t * P : (t + 1) * P],
                    rhs=x_codes[:, s : s + HALF].bitcast(FP8X4),
                    rhs_scale=x_scales[:, s : s + HALF],
                    start=True,
                    stop=True,
                )
            return acc

        def relu_on_scalar(acc, s):
            nc.scalar.activation(h_bf[:, s : s + HALF, :], acc[:].rearrange("p t w -> p w t"), RELU)

        def relu_on_vector(acc, s):
            nc.vector.tensor_scalar_max(h_bf[:, s : s + HALF, :], acc[:].rearrange("p t w -> p w t"), 0.0)

        def first_layer(c):
            s = c * CHUNK
            relu_on_scalar(hidden(s), s)
            bank = hidden(s + HALF)
            relu_on_scalar(bank, s + HALF)
            quantise(h_codes, h_scales, h_bf, s, CHUNK)
            return bank[:].rearrange("p t w -> p (t w)")

        def second_layer(b, s, n, y, copy=nc.scalar.copy, acc=None):
            if acc is None:
                acc = out_psum.tile([P, BANK], F32, name="out_acc")
            nc.tensor.matmul_mx(
                out=acc[:, 0:n],
                lhsT=w2_codes[:, b * P : (b + 1) * P].bitcast(FP8X4),
                lhsT_scale=w2_scales[:, b * P : (b + 1) * P],
                rhs=h_codes[:, s : s + n].bitcast(FP8X4),
                rhs_scale=h_scales[:, s : s + n],
                start=True,
                stop=True,
            )
            copy(y, acc[:, 0:n])

        def scatter(b, s, n, y):
            nc.vector.tensor_tensor(
                window[b][:].indirect(offsets[:, s // 16 : (s + n) // 16]), y, gates[:, s : s + n], MULT
            )

        y0 = held.tile([P, S], F32, name="y0")
        y1_first = held.tile([P, CHUNK], F32, name="y1_first")
        y2 = held.tile([P, S], F32, name="y2")

        interleave(nc.vector.tensor_copy, x_bf, x_raw[0], 0, 0, HALF)
        interleave(nc.scalar.copy, x_bf, x_raw[0], HALF, HALF, HALF)
        quantise(x_codes, x_scales, x_bf, 0, CHUNK)
        w1_by_slot = w1_raw[:].rearrange("p j (m t) -> p m t j", t=PACK)
        w1_columns = w1_bf[:].rearrange("p t m j -> p (t m) j")
        nc.vector.tensor_copy(w1_bf[:, 0:2].rearrange("p t m j -> p m t j"), w1_by_slot[:, :, 0:2, :])
        nc.scalar.copy(w1_bf[:, 3], w1_by_slot[:, :, 3, :])
        nc.vector.tensor_copy(w1_bf[:, 2], w1_by_slot[:, :, 2, :])
        quantise(w1_codes, w1_scales, w1_columns, 0, H // 2)
        quantise(w1_codes, w1_scales, w1_columns, H // 2, H // 2)
        halves = [hidden(i * HALF) for i in range(2)]
        for i in range(2):
            relu_on_vector(halves[i], i * HALF)
        prepare_w2(nc.vector.tensor_copy, 0)
        for i in range(2):
            quantise(h_codes, h_scales, h_bf, i * HALF, HALF)
        for i in range(2):
            second_layer(0, i * HALF, HALF, y0[:, i * HALF : (i + 1) * HALF], nc.vector.tensor_copy)
        nc.vector.memset(window[2][:, : T // 2], 0.0)
        scatter(0, 0, CHUNK, y0[:, 0:CHUNK])

        prepare_w2(nc.scalar.copy, 1)
        prepare_x(1)
        second_layer(1, 0, CHUNK, y1_first[:])
        scatter(1, 0, CHUNK, y1_first[:])
        first_layer(1)
        prepare_w2(nc.scalar.copy, 2)
        second_layer(2, 0, CHUNK, y2[:, 0:CHUNK])
        scatter(2, 0, CHUNK, y2[:, 0:CHUNK])
        prepare_x(2)
        prepare_w2(nc.scalar.copy, 3)
        y3 = held.tile([P, S], F32, name="y3", tag="x_bytes2")
        second_layer(3, 0, CHUNK, y3[:, 0:CHUNK])
        scatter(3, 0, CHUNK, y3[:, 0:CHUNK])

        second_layer(0, CHUNK, CHUNK, y0[:, CHUNK : 2 * CHUNK])
        scatter(0, CHUNK, CHUNK, y0[:, CHUNK : 2 * CHUNK])
        first_layer(2)
        prepare_x(3)
        y1 = held.tile([P, S - CHUNK], F32, name="y1", tag="x_bytes3")
        second_layer(1, CHUNK, CHUNK, y1[:, 0:CHUNK])
        scatter(1, CHUNK, CHUNK, y1[:, 0:CHUNK])
        second_layer(2, CHUNK, 2 * CHUNK, y2[:, CHUNK : 3 * CHUNK])
        scatter(2, CHUNK, 2 * CHUNK, y2[:, CHUNK : 3 * CHUNK])
        bank = first_layer(3)
        second_layer(3, CHUNK, 2 * CHUNK, y3[:, CHUNK : 3 * CHUNK], acc=bank)
        scatter(3, CHUNK, 2 * CHUNK, y3[:, CHUNK : 3 * CHUNK])

        rest = (
            (2, 3 * CHUNK, CHUNK, y2[:, 3 * CHUNK :]),
            (3, 3 * CHUNK, CHUNK, y3[:, 3 * CHUNK :]),
            (0, 2 * CHUNK, 2 * CHUNK, y0[:, 2 * CHUNK :]),
            (1, 2 * CHUNK, 2 * CHUNK, y1[:, CHUNK:]),
        )
        for b, s, n, y in rest:
            second_layer(b, s, n, y)
        for b, s, n, y in rest:
            scatter(b, s, n, y)
            nc.sync.dma_start(out[b * P : (b + 1) * P, :], window[b][:])
